import numpy as np
import ml_dtypes


def mxq(x, axis, fmt="e4m3"):
    dtype, down = {"e4m3": (ml_dtypes.float8_e4m3fn, 7), "e5m2": (ml_dtypes.float8_e5m2, 14)}[fmt]
    v = np.moveaxis(np.asarray(x, np.float32).astype(ml_dtypes.bfloat16).astype(np.float64), axis, -1)
    blocks = v.reshape(v.shape[:-1] + (-1, 32))
    amax = np.abs(blocks).max(-1, keepdims=True)
    byte = np.maximum(np.where(amax > 0, np.frexp(amax)[1] - 1 + 127, 0) - down, 1)
    scale = np.exp2(byte - 127.0)
    codes = (blocks / scale).astype(np.float32).astype(dtype).astype(np.float64)
    return np.moveaxis((codes * scale).reshape(v.shape), -1, axis)


WIDE = False


def mx_kscale(k):
    if not WIDE:
        return np.ones(k)
    levels = np.array([10, -10, 5, -5, 0])
    if k % 512:
        return np.exp2(np.random.permutation(np.resize(levels, k // 32))).repeat(32)
    a = np.empty((k // 512, 16))
    for p in range(k // 512):
        a[p, :8] = np.random.permutation(np.resize(levels, 8))
        for g in range(8):
            far = levels[np.abs(levels - a[p, g]) >= 10]
            a[p, g + 8] = far[np.random.randint(len(far))]
    return np.exp2(a.ravel()).repeat(32)


def f64(x):
    return np.asarray(x).astype(np.float64)


def striped(idx):
    return np.tile(idx.reshape(-1, 16).T, (8, 1)).astype(np.uint16)


def unstriped(offs):
    return offs[:16].T.reshape(-1).astype(np.int64)


E2M1 = np.array([0.0, 0.5, 1.0, 1.5, 2.0, 3.0, 4.0, 6.0, -0.0, -0.5, -1.0, -1.5, -2.0, -3.0, -4.0, -6.0])


def pack_weight(w, fmt):
    k, n = w.shape
    w = f64(np.asarray(w, np.float32).astype(ml_dtypes.bfloat16)).reshape(k // 32, 32, n)
    amax = np.abs(w).max(1)
    if fmt == "e4m3":
        byte = np.frexp(amax)[1] - 1 + 127 - 7
    else:
        mant, ex = np.frexp(amax / 6.0)
        byte = np.where(mant > 0.5, ex, ex - 1) + 127
    byte = np.clip(np.where(amax > 0, byte, 1), 1, 254)
    scaled = (w * np.exp2(127.0 - byte)[:, None, :]).reshape(k, n).astype(np.float32)
    by_word = np.ascontiguousarray(scaled.reshape(k // 512, 128, 4, n).transpose(0, 1, 3, 2))
    if fmt == "e4m3":
        words = by_word.astype(ml_dtypes.float8_e4m3fn).view(np.uint8)
    else:
        c = by_word.astype(ml_dtypes.float4_e2m1fn).view(np.uint8) & 0xF
        words = (c[..., 0::2] | (c[..., 1::2] << 4)).reshape(k // 512, 128, 2 * n)
    return np.ascontiguousarray(words), np.ascontiguousarray(byte.astype(np.uint8).reshape(k // 512, 16, n))


def unpack_weight(words, scales, fmt):
    g, _, n = scales.shape
    words = np.ascontiguousarray(words).reshape(g, 128, n, -1)
    if fmt == "e4m3":
        vals = words.view(ml_dtypes.float8_e4m3fn).astype(np.float64)
    else:
        nib = np.empty((g, 128, n, 4), np.uint8)
        nib[..., 0::2] = words & 0xF
        nib[..., 1::2] = words >> 4
        vals = E2M1[nib]
    vals = vals * np.repeat(np.exp2(scales.astype(np.float64) - 127.0), 8, axis=1)[..., None]
    return vals.transpose(0, 1, 3, 2).reshape(g * 512, n)


def gelu(v):
    return 0.5 * v * (1.0 + np.tanh(np.sqrt(2.0 / np.pi) * (v + 0.044715 * v**3)))


def bf(x):
    return np.asarray(x, np.float32).astype(ml_dtypes.bfloat16)

def planes(Y):
    n, m = Y.shape
    b = f64(bf(Y)).reshape(n // 32, 32, m)
    amax = np.abs(b).max(1)
    byte = np.clip(np.where(amax > 0, np.frexp(amax)[1] - 1 + 127 - 7, 1), 1, 254)
    codes = (b * np.exp2(127.0 - byte)[:, None, :]).reshape(n, m).astype(np.float32).astype(ml_dtypes.float8_e4m3fn).view(np.uint8)
    words = codes.reshape(n // 512, 128, 4, m).transpose(0, 1, 3, 2)
    return np.ascontiguousarray(words), np.ascontiguousarray(byte.astype(np.uint8).reshape(n // 512, 16, m))


K, T, S, H, N, T2, P = 1536, 2048, 1024, 1024, 512, 2048, 128

def setup_inputs():
    n = np.random.standard_normal
    s = mx_kscale(K)[:, None]
    u = mx_kscale(H)[:, None]
    od = -np.log(np.random.uniform(0.02, 1.0, (K, T)))
    tab_words, tab_scales = pack_weight(od * s, "e4m3")
    w4_words, w4_scales = pack_weight(n((K, H)) / np.sqrt(K) / s * u.T, "e2m1")
    return {
        "tab_words": tab_words, "tab_scales": tab_scales,
        "offs": striped(np.random.permutation(T)[:S]),
        "w4_words": w4_words, "w4_scales": w4_scales,
        "bu": (0.3 * n(H) * u[:, 0]).astype(np.float32),
        "wr": (0.5 * n((H, N)) / np.sqrt(H) / u).astype(np.float32),
        "lg": (0.8 * n(N)).astype(np.float32),
        "wgo": np.exp(0.3 * n((P, S))).astype(np.float32),
        "offs2": striped(np.random.permutation(T2)[:S]),
    }

def reference(tab_words, tab_scales, offs, w4_words, w4_scales, bu, wr, lg, wgo, offs2):
    v = unpack_weight(tab_words, tab_scales, "e4m3")[:, unstriped(offs)]
    w4 = unpack_weight(w4_words, w4_scales, "e2m1")
    c = np.maximum((w4.T @ v) + f64(bu)[:, None], 0.0)
    d = mxq(f64(wr), 0, "e4m3").T @ mxq(c, 0, "e4m3")
    y = np.exp(f64(lg)[:, None] - d)
    page = np.zeros((N, T2))
    page[:, unstriped(offs2)] = np.tile(f64(wgo), (N // P, 1)) * y
    y = page
    words, scales = planes(y)
    return y, words, scales

@@ -1,0 +1,304 @@
+from contextlib import ExitStack
+
+import concourse.mybir as mybir
+from concourse.masks import make_identity
+
+K, T, S, H, N, T2, P = 1536, 2048, 1024, 1024, 512, 2048, 128
+FLOPS = 2 * K * H * S + 2 * H * N * S
+
+F32 = mybir.dt.float32
+BF16 = mybir.dt.bfloat16
+I32 = mybir.dt.int32
+U32 = mybir.dt.uint32
+U16 = mybir.dt.uint16
+U8 = mybir.dt.uint8
+E4M3 = mybir.dt.float8_e4m3fn_x4
+E2M1 = mybir.dt.float4_e2m1fn_x4
+ACT = mybir.ActivationFunctionType
+MULT = mybir.AluOpType.mult
+
+PACK = 4
+KP = P * PACK
+PASSES1 = K // KP
+PASSES2 = H // KP
+BANK = 512
+CHUNKS = [(0, 256), (256, 256), (512, 512)]
+QUARTER = T2 // 4
+
+
+def tile_list_stain_remix_page_kernel(
+    tc, tab_words, tab_scales, offs, w4_words, w4_scales, bu, wr, lg, wgo, offs2, out_0, out_1, out_2
+):
+    nc = tc.nc
+    with ExitStack() as ctx:
+        keep = ctx.enter_context(tc.tile_pool(name="keep", bufs=1))
+        ring = ctx.enter_context(tc.tile_pool(name="ring", bufs=4))
+        psum = ctx.enter_context(tc.psum_pool(name="psum", bufs=1))
+
+        def bank(i):
+            return psum.tile([P, BANK], F32, name="bank%d" % i, tag="bank%d" % i)
+
+        def entries(tile, start, width):
+            return tile[:, start // 16 : (start + width) // 16]
+
+        tab_sc = keep.tile([P, T], U8, name="tab_sc")
+        nc.gpsimd.memset(tab_sc[:].bitcast(I32), 0)
+        w4_sc_raw = keep.tile([P, PASSES1 * H], U8, name="w4_sc_raw")
+        nc.vector.memset(w4_sc_raw[:].bitcast(I32), 0)
+        warm_in = keep.tile([P, 1], F32, name="warm_in")
+        warm_out = keep.tile([P, 1], F32, name="warm_out")
+        nc.gpsimd.memset(warm_in[:], 0.0)
+        nc.scalar.activation(out=warm_out[:], in_=warm_in[:], func=ACT.Exp)
+        bu_rows = keep.tile([P, P], F32, name="bu_rows")
+        nc.gpsimd.memset(bu_rows[:], 0.0)
+        ident = keep.tile([P, P], F32, name="ident")
+        make_identity(nc, ident[:])
+        moved_sc = [keep.tile([P, S], U8, name="moved_sc%d" % a, align_bytes=64) for a in range(1, PASSES1)]
+        for plane in moved_sc:
+            nc.gpsimd.memset(plane[:].bitcast(I32), 0)
+        pages = [keep.tile([P, T2], F32, name="page%d" % u) for u in range(PACK)]
+        nc.vector.memset(pages[0][:, 0:1023], 0.0)
+        nc.vector.memset(pages[0][:, 1023:T2], 0.0)
+        for page in pages[1:]:
+            for half in range(2):
+                nc.gpsimd.memset(page[:, half * 1024 : (half + 1) * 1024], 0.0)
+
+        idx = keep.tile([P, S // 16], U16, name="idx")
+        nc.sync.dma_start(idx[:], offs)
+        tab = [keep.tile([P, T], U32, name="tab%d" % a) for a in range(PASSES1)]
+
+        def load_tab(a):
+            nc.sync.dma_start(tab[a][:].bitcast(I32), tab_words[a].rearrange("p t i -> p (t i)").bitcast(I32))
+
+        load_tab(0)
+        for q in range(4):
+            nc.scalar.dma_start(
+                tab_sc[32 * q : 32 * q + 4 * PASSES1, :].bitcast(I32), tab_scales[:, 4 * q : 4 * q + 4, :].bitcast(I32)
+            )
+        w4_raw = keep.tile([P, PASSES1, H // 2], I32, name="w4_raw")
+        nc.sync.dma_start(w4_raw[:], w4_words.bitcast(I32).rearrange("a p w -> p a w"))
+        for q in range(4):
+            nc.sync.dma_start(
+                w4_sc_raw[32 * q : 32 * q + 4, :].bitcast(I32).rearrange("r (a w) -> r a w", a=PASSES1),
+                w4_scales[:, 4 * q : 4 * q + 4, :].bitcast(I32).rearrange("a r w -> r a w"),
+            )
+        load_tab(1)
+        load_tab(2)
+        for b in range(PASSES2):
+            nc.sync.dma_start(
+                bu_rows[PACK * b : PACK * (b + 1), :].rearrange("t (g i) -> t g i", i=8),
+                bu[KP * b : KP * (b + 1)].rearrange("(g t i) -> t g i", t=PACK, i=8),
+            )
+        lg_cols = keep.tile([P, PACK], F32, name="lg_cols")
+        nc.sync.dma_start(lg_cols[:], lg.rearrange("(p u) -> p u", u=PACK))
+        wr_raw = [keep.tile([P, PACK, N], F32, name="wr_raw%d" % b) for b in range(PASSES2)]
+        for b in range(PASSES2):
+            rows = wr[KP * b : KP * (b + 1), :].rearrange("(g t i) n -> t g i n", t=PACK, i=8)
+            for t in range(PACK):
+                nc.sync.dma_start(wr_raw[b][:, t, :], rows[t])
+        idx2 = keep.tile([P, S // 16], U16, name="idx2")
+        nc.sync.dma_start(idx2[:], offs2)
+        wgo_dealt = []
+        wgo_rows = wgo.rearrange("(q u) j -> q u j", u=PACK)
+        for c, (start, width) in enumerate(CHUNKS):
+            dealt = keep.tile([P, PACK, width], F32, name="wgo%d" % c)
+            for q in (0, 2, 1, 3):
+                nc.sync.dma_start(dealt[32 * q : 32 * (q + 1), :, :], wgo_rows[:, :, start : start + width])
+            wgo_dealt.append(dealt)
+
+        bu_bank = bank(7)
+        nc.tensor.transpose(bu_bank[:, 0:P], bu_rows[:], ident[:])
+        bu_cols = keep.tile([P, PACK * PASSES2], F32, name="bu_cols")
+        nc.scalar.copy(out=bu_cols[:], in_=bu_bank[:, 0 : PACK * PASSES2])
+
+        got_sc = keep.tile([P, S], U8, name="got_sc", align_bytes=64)
+        nc.vector.tensor_copy(out=got_sc[:], in_=tab_sc[:].indirect(idx[:]))
+        for a in range(1, PASSES1):
+            nc.gpsimd.dma_start(moved_sc[a - 1][0:112, :].bitcast(I32), got_sc[4 * a : 4 * a + 112, :].bitcast(I32))
+        v_scales = [got_sc] + moved_sc
+
+        w4 = keep.tile([P, PASSES1 * 2 * H], U8, name="w4", align_bytes=64)
+        nc.vector.tensor_copy(
+            out=w4[:].bitcast(I32).rearrange("p (ab t g w) -> p ab t g w", t=PACK, g=16, w=4),
+            in_=w4_raw[:].rearrange("p a (b g t w) -> p (a b) t g w", t=PACK, g=16, w=4),
+        )
+        w4_sc = keep.tile([P, PASSES1 * H], U8, name="w4_sc", align_bytes=64)
+        nc.vector.tensor_copy(
+            out=w4_sc[:].bitcast(I32).rearrange("p (ab t g w) -> p ab t g w", t=PACK, g=16, w=2),
+            in_=w4_sc_raw[:].bitcast(I32).rearrange("p (ab g t w) -> p ab t g w", t=PACK, g=16, w=2),
+        )
+
+        v_words = {}
+
+        def gather(c, a):
+            start, width = CHUNKS[c]
+            tag = "got0_1" if (c, a) == (2, 1) else "got%d_%d" % (c, a)
+            got = keep.tile([P, width], U32, name=tag, tag=tag, align_bytes=64)
+            nc.vector.tensor_copy(out=got[:], in_=tab[a][:].indirect(entries(idx, start, width)))
+            v_words[c, a] = got
+
+        def unmix_pass(c, a, s, out, first, last):
+            start, width = CHUNKS[c]
+            step = BANK if width == BANK else P
+            col = a * H + s * P
+            for j in range(0, width, step):
+                nc.tensor.matmul_mx(
+                    out=out[:, j : j + step],
+                    lhsT=w4[:, 2 * col : 2 * (col + P)].bitcast(E2M1),
+                    lhsT_scale=w4_sc[:, col : col + P],
+                    rhs=v_words[c, a][:, j : j + step].bitcast(E4M3),
+                    rhs_scale=v_scales[a][:, start + j : start + j + step],
+                    start=first and j == 0,
+                    stop=last and j + step == width,
+                )
+
+        sums = {}
+
+        def unmix(c, banks):
+            width = CHUNKS[c][1]
+            per_bank = BANK // width
+            tiles = [bank(i) for i in banks]
+            for s in range(PACK * PASSES2):
+                sums[c, s] = tiles[s // per_bank][:, (s % per_bank) * width : (s % per_bank + 1) * width]
+            if per_bank > 1:
+                order = [(a, s) for a in range(PASSES1) for s in range(PACK * PASSES2)]
+            else:
+                order = [(a, s) for s in range(PACK * PASSES2) for a in range(PASSES1)]
+            for a, s in order:
+                unmix_pass(
+                    c, a, s, sums[c, s], a == 0 and s % per_bank == 0, a == PASSES1 - 1 and s % per_bank == per_bank - 1
+                )
+
+        staged = {}
+
+        def rectify(c, b):
+            width = CHUNKS[c][1]
+            if (c, b) == (2, 1):
+                stage = keep.tile([P, PACK, width], BF16, name="held", tag="held")
+            else:
+                stage = ring.tile([P, PACK, width], BF16, name="stage", tag="stage")
+            for t in range(PACK):
+                s = PACK * b + t
+                nc.scalar.activation(out=stage[:, t, :], in_=sums[c, s], func=ACT.Relu, bias=bu_cols[:, s : s + 1])
+            staged[c, b] = stage
+
+        def weave(engine, stage, width):
+            woven = ring.tile([P, width * PACK], BF16, name="woven", tag="woven", align_bytes=64)
+            dst = woven[:].rearrange("p (c i t) -> p c t i", i=4, t=PACK)
+            src = stage[:].rearrange("p t (c i) -> p c t i", i=4)
+            if engine == "vector":
+                nc.vector.tensor_copy(out=dst, in_=src)
+            else:
+                nc.scalar.copy(out=dst, in_=src)
+            return woven
+
+        def quantise(woven, width, name):
+            codes = keep.tile([P, width], U32, name=name + "_codes", align_bytes=64)
+            scales = keep.tile([P, width], U8, name=name + "_scales", align_bytes=64)
+            nc.vector.quantize_mx(out=codes[:].bitcast(E4M3), scales=scales[:], in_=woven[:])
+            return codes, scales
+
+        wr_q = {}
+
+        def prepare_wr(b):
+            woven = ring.tile([P, N * PACK], BF16, name="woven", tag="woven", align_bytes=64)
+            copy = nc.scalar.copy if b == 0 else nc.vector.tensor_copy
+            copy(
+                out=woven[:].rearrange("p (u m t) -> p m t u", u=PACK, t=PACK),
+                in_=wr_raw[b][:].rearrange("p t (m u) -> p m t u", u=PACK),
+            )
+            wr_q[b] = quantise(woven, N, "wr%d" % b)
+
+        c_q = {}
+
+        def quantise_c(c, b, engine):
+            width = CHUNKS[c][1]
+            c_q[c, b] = quantise(weave(engine, staged[c, b], width), width, "c%d_%d" % (c, b))
+
+        light = {}
+
+        def remix(c, banks):
+            width = CHUNKS[c][1]
+            per_bank = BANK // width
+            tiles = [bank(i) for i in banks]
+            for u in range(PACK):
+                d = tiles[u // per_bank][:, (u % per_bank) * width : (u % per_bank + 1) * width]
+                for b in range(PASSES2):
+                    nc.tensor.matmul_mx(
+                        out=d,
+                        lhsT=wr_q[b][0][:, u * P : (u + 1) * P].bitcast(E4M3),
+                        lhsT_scale=wr_q[b][1][:, u * P : (u + 1) * P],
+                        rhs=c_q[c, b][0][:].bitcast(E4M3),
+                        rhs_scale=c_q[c, b][1][:],
+                        start=b == 0,
+                        stop=b == PASSES2 - 1,
+                    )
+                sums["d", c, u] = d
+
+        def transmit(c, u):
+            width = CHUNKS[c][1]
+            tag = "held" if (c, u) == (1, 3) else "y%d_%d" % (c, u)
+            y = keep.tile([P, width], F32, name=tag, tag=tag)
+            nc.scalar.activation(out=y[:], in_=sums["d", c, u], func=ACT.Exp, scale=-1.0, bias=lg_cols[:, u : u + 1])
+            light[c, u] = y
+
+        def scatter(c, u):
+            start, width = CHUNKS[c]
+            nc.vector.tensor_tensor(
+                out=pages[u][:].indirect(entries(idx2, start, width)),
+                in0=light[c, u][:],
+                in1=wgo_dealt[c][:, u, :],
+                op=MULT,
+            )
+
+        for a in range(PASSES1):
+            gather(0, a)
+        unmix(0, [0, 1, 2, 3])
+        for a in range(PASSES1):
+            gather(1, a)
+        unmix(1, [4, 5, 6, 7])
+        for a in range(PASSES1):
+            gather(2, a)
+        for b in range(PASSES2):
+            prepare_wr(b)
+            rectify(0, b)
+            quantise_c(0, b, "vector")
+        remix(0, [0, 1])
+        for b in range(PASSES2):
+            rectify(1, b)
+            quantise_c(1, b, "vector")
+        for u in range(PACK):
+            transmit(0, u)
+            scatter(0, u)
+        remix(1, [0, 1])
+        unmix(2, [2, 3, 4, 5, 6, 7, 2, 3])
+        for u in range(PACK - 1):
+            transmit(1, u)
+            scatter(1, u)
+        for b in range(PASSES2):
+            rectify(2, b)
+            quantise_c(2, b, "scalar")
+        transmit(1, PACK - 1)
+        scatter(1, PACK - 1)
+        remix(2, [4, 5, 6, 7])
+
+        out_rows = out_0.rearrange("(p u) m -> p u m", u=PACK)
+        page_stage = [ring.tile([P, PACK, QUARTER], BF16, name="stage", tag="stage") for q in range(4)]
+        for u in range(PACK):
+            transmit(2, u)
+            scatter(2, u)
+            nc.sync.dma_start(out_rows[:, u, :], pages[u][:])
+            for q in range(4):
+                nc.scalar.copy(out=page_stage[q][:, u, :], in_=pages[u][:, q * QUARTER : (q + 1) * QUARTER])
+
+        out_words = out_1[0].rearrange("p m t -> p (m t)").bitcast(I32)
+        y_scales = keep.tile([P, T2], U8, name="y_scales", align_bytes=64)
+        for q in range(4):
+            cols = slice(q * QUARTER, (q + 1) * QUARTER)
+            woven = weave("scalar" if q == 3 else "vector", page_stage[q], QUARTER)
+            y_codes = keep.tile([P, QUARTER], U32, name="y_codes%d" % q, align_bytes=64)
+            nc.vector.quantize_mx(out=y_codes[:].bitcast(E4M3), scales=y_scales[:, cols], in_=woven[:])
+            nc.sync.dma_start(out_words[:, cols], y_codes[:].bitcast(I32))
+        for q in range(4):
+            queue = nc.sync if q % 2 == 0 else nc.scalar
+            queue.dma_start(out_2[0, 4 * q : 4 * q + 4, :].bitcast(I32), y_scales[32 * q : 32 * q + 4, :].bitcast(I32))

@@ -41,7 +41,7 @@ def tile_list_stain_remix_page_kernel(
         def entries(tile, start, width):
             return tile[:, start // 16 : (start + width) // 16]
 
-        tab_sc = keep.tile([P, T], U8, name="tab_sc")
+        tab_sc = keep.tile([P, T], U8, name="tab_sc", align_bytes=64)
         nc.gpsimd.memset(tab_sc[:].bitcast(I32), 0)
         w4_sc_raw = keep.tile([P, PASSES1 * H], U8, name="w4_sc_raw")
         nc.vector.memset(w4_sc_raw[:].bitcast(I32), 0)
@@ -57,9 +57,10 @@ def tile_list_stain_remix_page_kernel(
         for plane in moved_sc:
             nc.gpsimd.memset(plane[:].bitcast(I32), 0)
         pages = [keep.tile([P, T2], F32, name="page%d" % u) for u in range(PACK)]
-        nc.vector.memset(pages[0][:, 0:1023], 0.0)
-        nc.vector.memset(pages[0][:, 1023:T2], 0.0)
-        for page in pages[1:]:
+        for page in pages[:2]:
+            nc.vector.memset(page[:, 0:1023], 0.0)
+            nc.vector.memset(page[:, 1023:T2], 0.0)
+        for page in pages[2:]:
             for half in range(2):
                 nc.gpsimd.memset(page[:, half * 1024 : (half + 1) * 1024], 0.0)
 
@@ -75,7 +76,7 @@ def tile_list_stain_remix_page_kernel(
             nc.scalar.dma_start(
                 tab_sc[32 * q : 32 * q + 4 * PASSES1, :].bitcast(I32), tab_scales[:, 4 * q : 4 * q + 4, :].bitcast(I32)
             )
-        w4_raw = keep.tile([P, PASSES1, H // 2], I32, name="w4_raw")
+        w4_raw = keep.tile([P, PASSES1, H // 2], I32, name="w4_raw", align_bytes=64)
         nc.sync.dma_start(w4_raw[:], w4_words.bitcast(I32).rearrange("a p w -> p a w"))
         for q in range(4):
             nc.sync.dma_start(
@@ -132,8 +133,8 @@ def tile_list_stain_remix_page_kernel(
 
         def gather(c, a):
             start, width = CHUNKS[c]
-            tag = "got0_1" if (c, a) == (2, 1) else "got%d_%d" % (c, a)
-            got = keep.tile([P, width], U32, name=tag, tag=tag, align_bytes=64)
+            tag = {(1, 0): "tab_sc", (2, 0): "w4_raw"}.get((c, a), "got%d_%d" % (c, a))
+            got = keep.tile([P, width], U32, name="got%d_%d" % (c, a), tag=tag, align_bytes=64)
             nc.vector.tensor_copy(out=got[:], in_=tab[a][:].indirect(entries(idx, start, width)))
             v_words[c, a] = got
 
@@ -202,8 +203,7 @@ def tile_list_stain_remix_page_kernel(
 
         def prepare_wr(b):
             woven = ring.tile([P, N * PACK], BF16, name="woven", tag="woven", align_bytes=64)
-            copy = nc.scalar.copy if b == 0 else nc.vector.tensor_copy
-            copy(
+            nc.vector.tensor_copy(
                 out=woven[:].rearrange("p (u m t) -> p m t u", u=PACK, t=PACK),
                 in_=wr_raw[b][:].rearrange("p t (m u) -> p m t u", u=PACK),
             )
@@ -264,12 +264,12 @@ def tile_list_stain_remix_page_kernel(
             rectify(0, b)
             quantise_c(0, b, "vector")
         remix(0, [0, 1])
-        for b in range(PASSES2):
-            rectify(1, b)
-            quantise_c(1, b, "vector")
         for u in range(PACK):
             transmit(0, u)
             scatter(0, u)
+        for b in range(PASSES2):
+            rectify(1, b)
+            quantise_c(1, b, "vector")
         remix(1, [0, 1])
         unmix(2, [2, 3, 4, 5, 6, 7, 2, 3])
         for u in range(PACK - 1):
@@ -289,13 +289,24 @@ def tile_list_stain_remix_page_kernel(
             scatter(2, u)
             nc.sync.dma_start(out_rows[:, u, :], pages[u][:])
             for q in range(4):
-                nc.scalar.copy(out=page_stage[q][:, u, :], in_=pages[u][:, q * QUARTER : (q + 1) * QUARTER])
+                copy = nc.vector.tensor_copy if u == PACK - 1 and q < 3 else nc.scalar.copy
+                copy(out=page_stage[q][:, u, :], in_=pages[u][:, q * QUARTER : (q + 1) * QUARTER])
 
         out_words = out_1[0].rearrange("p m t -> p (m t)").bitcast(I32)
         y_scales = keep.tile([P, T2], U8, name="y_scales", align_bytes=64)
-        for q in range(4):
+        for q in (0, 1, 3, 2):
             cols = slice(q * QUARTER, (q + 1) * QUARTER)
-            woven = weave("scalar" if q == 3 else "vector", page_stage[q], QUARTER)
+            if q == 2:
+                woven = ring.tile([P, QUARTER * PACK], BF16, name="woven", tag="woven", align_bytes=64)
+                for copy, cut in ((nc.vector.tensor_copy, 0), (nc.scalar.copy, QUARTER // 2)):
+                    copy(
+                        out=woven[:, cut * PACK : (cut + QUARTER // 2) * PACK].rearrange(
+                            "p (c i t) -> p c t i", i=4, t=PACK
+                        ),
+                        in_=page_stage[q][:, :, cut : cut + QUARTER // 2].rearrange("p t (c i) -> p c t i", i=4),
+                    )
+            else:
+                woven = weave("scalar" if q == 3 else "vector", page_stage[q], QUARTER)
             y_codes = keep.tile([P, QUARTER], U32, name="y_codes%d" % q, align_bytes=64)
             nc.vector.quantize_mx(out=y_codes[:].bitcast(E4M3), scales=y_scales[:, cols], in_=woven[:])
             nc.sync.dma_start(out_words[:, cols], y_codes[:].bitcast(I32))

@@ -283,32 +283,32 @@ def tile_list_stain_remix_page_kernel(
         remix(2, [4, 5, 6, 7])
 
         out_rows = out_0.rearrange("(p u) m -> p u m", u=PACK)
-        page_stage = [ring.tile([P, PACK, QUARTER], BF16, name="stage", tag="stage") for q in range(4)]
+        pairs = [ring.tile([P, 2, QUARTER, 2], BF16, name="stage", tag="stage") for q in range(4)]
         for u in range(PACK):
             transmit(2, u)
             scatter(2, u)
+        for u in range(PACK):
             nc.sync.dma_start(out_rows[:, u, :], pages[u][:])
             for q in range(4):
-                copy = nc.vector.tensor_copy if u == PACK - 1 and q < 3 else nc.scalar.copy
-                copy(out=page_stage[q][:, u, :], in_=pages[u][:, q * QUARTER : (q + 1) * QUARTER])
+                copy = nc.vector.tensor_copy if u >= 2 and q == 0 else nc.scalar.copy
+                copy(out=pairs[q][:, u // 2, :, u % 2], in_=pages[u][:, q * QUARTER : (q + 1) * QUARTER])
 
         out_words = out_1[0].rearrange("p m t -> p (m t)").bitcast(I32)
         y_scales = keep.tile([P, T2], U8, name="y_scales", align_bytes=64)
-        for q in (0, 1, 3, 2):
+        page_woven = []
+        for q in range(4):
+            woven = ring.tile([P, QUARTER * PACK], BF16, name="woven", tag="woven", align_bytes=64)
+            words = pairs[q][:].rearrange("p h m e -> p (h m e)")
+            copy, word = (nc.vector.tensor_copy, I32) if q < 3 else (nc.scalar.copy, U32)
+            copy(
+                out=woven[:].bitcast(word).rearrange("p (m h) -> p m h", h=2),
+                in_=words.bitcast(word).rearrange("p (h m) -> p m h", h=2),
+            )
+            page_woven.append(woven)
+        for q in range(4):
             cols = slice(q * QUARTER, (q + 1) * QUARTER)
-            if q == 2:
-                woven = ring.tile([P, QUARTER * PACK], BF16, name="woven", tag="woven", align_bytes=64)
-                for copy, cut in ((nc.vector.tensor_copy, 0), (nc.scalar.copy, QUARTER // 2)):
-                    copy(
-                        out=woven[:, cut * PACK : (cut + QUARTER // 2) * PACK].rearrange(
-                            "p (c i t) -> p c t i", i=4, t=PACK
-                        ),
-                        in_=page_stage[q][:, :, cut : cut + QUARTER // 2].rearrange("p t (c i) -> p c t i", i=4),
-                    )
-            else:
-                woven = weave("scalar" if q == 3 else "vector", page_stage[q], QUARTER)
             y_codes = keep.tile([P, QUARTER], U32, name="y_codes%d" % q, align_bytes=64)
-            nc.vector.quantize_mx(out=y_codes[:].bitcast(E4M3), scales=y_scales[:, cols], in_=woven[:])
+            nc.vector.quantize_mx(out=y_codes[:].bitcast(E4M3), scales=y_scales[:, cols], in_=page_woven[q][:])
             nc.sync.dma_start(out_words[:, cols], y_codes[:].bitcast(I32))
         for q in range(4):
             queue = nc.sync if q % 2 == 0 else nc.scalar

@@ -24,6 +24,7 @@ PASSES2 = H // KP
 BANK = 512
 CHUNKS = [(0, 256), (256, 256), (512, 512)]
 QUARTER = T2 // 4
+EIGHTH = T2 // 8
 
 
 def tile_list_stain_remix_page_kernel(
@@ -290,8 +291,10 @@ def tile_list_stain_remix_page_kernel(
         for u in range(PACK):
             nc.sync.dma_start(out_rows[:, u, :], pages[u][:])
             for q in range(4):
-                copy = nc.vector.tensor_copy if u >= 2 and q == 0 else nc.scalar.copy
-                copy(out=pairs[q][:, u // 2, :, u % 2], in_=pages[u][:, q * QUARTER : (q + 1) * QUARTER])
+                cuts = [(0, EIGHTH), (EIGHTH, QUARTER)] if u >= 2 and q == 0 else [(0, QUARTER)]
+                for lo, hi in cuts:
+                    copy = nc.vector.tensor_copy if hi == EIGHTH else nc.scalar.copy
+                    copy(out=pairs[q][:, u // 2, lo:hi, u % 2], in_=pages[u][:, q * QUARTER + lo : q * QUARTER + hi])
 
         out_words = out_1[0].rearrange("p m t -> p (m t)").bitcast(I32)
         y_scales = keep.tile([P, T2], U8, name="y_scales", align_bytes=64)
@@ -300,16 +303,20 @@ def tile_list_stain_remix_page_kernel(
             woven = ring.tile([P, QUARTER * PACK], BF16, name="woven", tag="woven", align_bytes=64)
             words = pairs[q][:].rearrange("p h m e -> p (h m e)")
             copy, word = (nc.vector.tensor_copy, I32) if q < 3 else (nc.scalar.copy, U32)
-            copy(
-                out=woven[:].bitcast(word).rearrange("p (m h) -> p m h", h=2),
-                in_=words.bitcast(word).rearrange("p (h m) -> p m h", h=2),
-            )
+            for lo, hi in [(0, QUARTER)] if q in (1, 2) else [(0, EIGHTH), (EIGHTH, QUARTER)]:
+                copy(
+                    out=woven[:].bitcast(word).rearrange("p (m h) -> p m h", h=2)[:, lo:hi, :],
+                    in_=words.bitcast(word).rearrange("p (h m) -> p m h", h=2)[:, lo:hi, :],
+                )
             page_woven.append(woven)
         for q in range(4):
-            cols = slice(q * QUARTER, (q + 1) * QUARTER)
-            y_codes = keep.tile([P, QUARTER], U32, name="y_codes%d" % q, align_bytes=64)
-            nc.vector.quantize_mx(out=y_codes[:].bitcast(E4M3), scales=y_scales[:, cols], in_=page_woven[q][:])
-            nc.sync.dma_start(out_words[:, cols], y_codes[:].bitcast(I32))
+            for lo, hi in [(0, QUARTER)] if q < 3 else [(0, EIGHTH), (EIGHTH, QUARTER)]:
+                cols = slice(q * QUARTER + lo, q * QUARTER + hi)
+                y_codes = keep.tile([P, hi - lo], U32, name="y_codes%d_%d" % (q, lo), align_bytes=64)
+                nc.vector.quantize_mx(
+                    out=y_codes[:].bitcast(E4M3), scales=y_scales[:, cols], in_=page_woven[q][:, PACK * lo : PACK * hi]
+                )
+                nc.sync.dma_start(out_words[:, cols], y_codes[:].bitcast(I32))
         for q in range(4):
             queue = nc.sync if q % 2 == 0 else nc.scalar
             queue.dma_start(out_2[0, 4 * q : 4 * q + 4, :].bitcast(I32), y_scales[32 * q : 32 * q + 4, :].bitcast(I32))

@@ -134,10 +134,14 @@ def tile_list_stain_remix_page_kernel(
 
         def gather(c, a):
             start, width = CHUNKS[c]
-            tag = {(1, 0): "tab_sc", (2, 0): "w4_raw"}.get((c, a), "got%d_%d" % (c, a))
+            tag = {(2, 0): "w4_raw"}.get((c, a), "got%d_%d" % (c, a))
+            if c == 1 and a > 0:
+                width = S - start
             got = keep.tile([P, width], U32, name="got%d_%d" % (c, a), tag=tag, align_bytes=64)
             nc.vector.tensor_copy(out=got[:], in_=tab[a][:].indirect(entries(idx, start, width)))
-            v_words[c, a] = got
+            v_words[c, a] = got[:, 0 : CHUNKS[c][1]]
+            if width > CHUNKS[c][1]:
+                v_words[c + 1, a] = got[:, CHUNKS[c][1] : width]
 
         def unmix_pass(c, a, s, out, first, last):
             start, width = CHUNKS[c]
@@ -184,8 +188,11 @@ def tile_list_stain_remix_page_kernel(
                 nc.scalar.activation(out=stage[:, t, :], in_=sums[c, s], func=ACT.Relu, bias=bu_cols[:, s : s + 1])
             staged[c, b] = stage
 
-        def weave(engine, stage, width):
-            woven = ring.tile([P, width * PACK], BF16, name="woven", tag="woven", align_bytes=64)
+        def weave(engine, stage, width, tag=None):
+            if tag:
+                woven = keep.tile([P, width * PACK], BF16, name="woven_" + tag, tag=tag, align_bytes=64)
+            else:
+                woven = ring.tile([P, width * PACK], BF16, name="woven", tag="woven", align_bytes=64)
             dst = woven[:].rearrange("p (c i t) -> p c t i", i=4, t=PACK)
             src = stage[:].rearrange("p t (c i) -> p c t i", i=4)
             if engine == "vector":
@@ -194,9 +201,9 @@ def tile_list_stain_remix_page_kernel(
                 nc.scalar.copy(out=dst, in_=src)
             return woven
 
-        def quantise(woven, width, name):
-            codes = keep.tile([P, width], U32, name=name + "_codes", align_bytes=64)
-            scales = keep.tile([P, width], U8, name=name + "_scales", align_bytes=64)
+        def quantise(woven, width, name, tag=None):
+            codes = keep.tile([P, width], U32, name=name + "_codes", tag=name + "_codes", align_bytes=64)
+            scales = keep.tile([P, width], U8, name=name + "_scales", tag=tag or name + "_scales", align_bytes=64)
             nc.vector.quantize_mx(out=codes[:].bitcast(E4M3), scales=scales[:], in_=woven[:])
             return codes, scales
 
@@ -214,7 +221,8 @@ def tile_list_stain_remix_page_kernel(
 
         def quantise_c(c, b, engine):
             width = CHUNKS[c][1]
-            c_q[c, b] = quantise(weave(engine, staged[c, b], width), width, "c%d_%d" % (c, b))
+            woven = weave(engine, staged[c, b], width, {(2, 1): "last"}.get((c, b)))
+            c_q[c, b] = quantise(woven, width, "c%d_%d" % (c, b))
 
         light = {}
 
@@ -238,8 +246,8 @@ def tile_list_stain_remix_page_kernel(
 
         def transmit(c, u):
             width = CHUNKS[c][1]
-            tag = "held" if (c, u) == (1, 3) else "y%d_%d" % (c, u)
-            y = keep.tile([P, width], F32, name=tag, tag=tag)
+            tag = {(1, 3): "held", (1, 2): "last"}.get((c, u), "y%d_%d" % (c, u))
+            y = keep.tile([P, width], F32, name="y%d_%d" % (c, u), tag=tag, align_bytes=None if tag == "held" else 64)
             nc.scalar.activation(out=y[:], in_=sums["d", c, u], func=ACT.Exp, scale=-1.0, bias=lg_cols[:, u : u + 1])
             light[c, u] = y
 
@@ -258,8 +266,7 @@ def tile_list_stain_remix_page_kernel(
         for a in range(PASSES1):
             gather(1, a)
         unmix(1, [4, 5, 6, 7])
-        for a in range(PASSES1):
-            gather(2, a)
+        gather(2, 0)
         for b in range(PASSES2):
             prepare_wr(b)
             rectify(0, b)
@@ -271,17 +278,19 @@ def tile_list_stain_remix_page_kernel(
         for b in range(PASSES2):
             rectify(1, b)
             quantise_c(1, b, "vector")
-        remix(1, [0, 1])
-        unmix(2, [2, 3, 4, 5, 6, 7, 2, 3])
-        for u in range(PACK - 1):
+        unmix(2, [2, 3, 4, 5, 6, 7, 0, 1])
+        rectify(2, 0)
+        remix(1, [2, 3])
+        for u in range(2):
             transmit(1, u)
             scatter(1, u)
-        for b in range(PASSES2):
-            rectify(2, b)
-            quantise_c(2, b, "scalar")
-        transmit(1, PACK - 1)
-        scatter(1, PACK - 1)
+        quantise_c(2, 0, "scalar")
+        rectify(2, 1)
+        quantise_c(2, 1, "scalar")
         remix(2, [4, 5, 6, 7])
+        for u in (3, 2):
+            transmit(1, u)
+            scatter(1, u)
 
         out_rows = out_0.rearrange("(p u) m -> p u m", u=PACK)
         pairs = [ring.tile([P, 2, QUARTER, 2], BF16, name="stage", tag="stage") for q in range(4)]

@@ -25,6 +25,8 @@ BANK = 512
 CHUNKS = [(0, 256), (256, 256), (512, 512)]
 QUARTER = T2 // 4
 EIGHTH = T2 // 8
+SLICES = PACK * PASSES2
+EDGE = 64
 
 
 def tile_list_stain_remix_page_kernel(
@@ -33,6 +35,7 @@ def tile_list_stain_remix_page_kernel(
     nc = tc.nc
     with ExitStack() as ctx:
         keep = ctx.enter_context(tc.tile_pool(name="keep", bufs=1))
+        laid = ctx.enter_context(tc.tile_pool(name="laid", bufs=1))
         ring = ctx.enter_context(tc.tile_pool(name="ring", bufs=4))
         psum = ctx.enter_context(tc.psum_pool(name="psum", bufs=1))
 
@@ -42,16 +45,22 @@ def tile_list_stain_remix_page_kernel(
         def entries(tile, start, width):
             return tile[:, start // 16 : (start + width) // 16]
 
-        tab_sc = keep.tile([P, T], U8, name="tab_sc", align_bytes=64)
+        at_wr_second = 0
+        at_tab_sc = at_wr_second + 4 * PACK * N - EDGE
+        at_wgo = at_tab_sc + T - EDGE
+
+        def lay(name, shape, dtype, at):
+            return laid.tile(shape, dtype, name=name, align_bytes=EDGE, offset=at)
+
+        bu_rows = keep.tile([P, P], F32, name="bu_rows")
+        nc.gpsimd.memset(bu_rows[:], 0.0)
+        tab_sc = lay("tab_sc", [P, T], U8, at_tab_sc)
         nc.gpsimd.memset(tab_sc[:].bitcast(I32), 0)
         w4_sc_raw = keep.tile([P, PASSES1 * H], U8, name="w4_sc_raw")
         nc.vector.memset(w4_sc_raw[:].bitcast(I32), 0)
         warm_in = keep.tile([P, 1], F32, name="warm_in")
         warm_out = keep.tile([P, 1], F32, name="warm_out")
-        nc.gpsimd.memset(warm_in[:], 0.0)
-        nc.scalar.activation(out=warm_out[:], in_=warm_in[:], func=ACT.Exp)
-        bu_rows = keep.tile([P, P], F32, name="bu_rows")
-        nc.gpsimd.memset(bu_rows[:], 0.0)
+        nc.vector.memset(warm_in[:], 0.0)
         ident = keep.tile([P, P], F32, name="ident")
         make_identity(nc, ident[:])
         moved_sc = [keep.tile([P, S], U8, name="moved_sc%d" % a, align_bytes=64) for a in range(1, PASSES1)]
@@ -73,10 +82,14 @@ def tile_list_stain_remix_page_kernel(
             nc.sync.dma_start(tab[a][:].bitcast(I32), tab_words[a].rearrange("p t i -> p (t i)").bitcast(I32))
 
         load_tab(0)
+        nc.scalar.dma_start(
+            bu_rows[0:SLICES, :].rearrange("s (g i) -> s g i", i=8), bu.rearrange("(g s i) -> s g i", s=SLICES, i=8)
+        )
         for q in range(4):
             nc.scalar.dma_start(
                 tab_sc[32 * q : 32 * q + 4 * PASSES1, :].bitcast(I32), tab_scales[:, 4 * q : 4 * q + 4, :].bitcast(I32)
             )
+        nc.scalar.activation(out=warm_out[:], in_=warm_in[:], func=ACT.Exp)
         w4_raw = keep.tile([P, PASSES1, H // 2], I32, name="w4_raw", align_bytes=64)
         nc.sync.dma_start(w4_raw[:], w4_words.bitcast(I32).rearrange("a p w -> p a w"))
         for q in range(4):
@@ -86,27 +99,16 @@ def tile_list_stain_remix_page_kernel(
             )
         load_tab(1)
         load_tab(2)
-        for b in range(PASSES2):
-            nc.sync.dma_start(
-                bu_rows[PACK * b : PACK * (b + 1), :].rearrange("t (g i) -> t g i", i=8),
-                bu[KP * b : KP * (b + 1)].rearrange("(g t i) -> t g i", t=PACK, i=8),
-            )
-        lg_cols = keep.tile([P, PACK], F32, name="lg_cols")
-        nc.sync.dma_start(lg_cols[:], lg.rearrange("(p u) -> p u", u=PACK))
-        wr_raw = [keep.tile([P, PACK, N], F32, name="wr_raw%d" % b) for b in range(PASSES2)]
-        for b in range(PASSES2):
-            rows = wr[KP * b : KP * (b + 1), :].rearrange("(g t i) n -> t g i n", t=PACK, i=8)
+        wr_raw = [keep.tile([P, PACK, N], F32, name="wr_raw0"), lay("wr_raw1", [P, PACK, N], F32, at_wr_second)]
+        wr_rows = wr.rearrange("(g s i) n -> s g i n", s=SLICES, i=8)
+
+        def load_wr(b):
             for t in range(PACK):
-                nc.sync.dma_start(wr_raw[b][:, t, :], rows[t])
+                nc.sync.dma_start(wr_raw[b][:, t, :], wr_rows[PACK * b + t])
+
+        load_wr(0)
         idx2 = keep.tile([P, S // 16], U16, name="idx2")
         nc.sync.dma_start(idx2[:], offs2)
-        wgo_dealt = []
-        wgo_rows = wgo.rearrange("(q u) j -> q u j", u=PACK)
-        for c, (start, width) in enumerate(CHUNKS):
-            dealt = keep.tile([P, PACK, width], F32, name="wgo%d" % c)
-            for q in (0, 2, 1, 3):
-                nc.sync.dma_start(dealt[32 * q : 32 * (q + 1), :, :], wgo_rows[:, :, start : start + width])
-            wgo_dealt.append(dealt)
 
         bu_bank = bank(7)
         nc.tensor.transpose(bu_bank[:, 0:P], bu_rows[:], ident[:])
@@ -116,18 +118,27 @@ def tile_list_stain_remix_page_kernel(
         got_sc = keep.tile([P, S], U8, name="got_sc", align_bytes=64)
         nc.vector.tensor_copy(out=got_sc[:], in_=tab_sc[:].indirect(idx[:]))
         for a in range(1, PASSES1):
-            nc.gpsimd.dma_start(moved_sc[a - 1][0:112, :].bitcast(I32), got_sc[4 * a : 4 * a + 112, :].bitcast(I32))
+            nc.sync.dma_start(moved_sc[a - 1][0:112, :].bitcast(I32), got_sc[4 * a : 4 * a + 112, :].bitcast(I32))
         v_scales = [got_sc] + moved_sc
+        load_wr(1)
+        lg_cols = lay("lg_cols", [P, PACK], F32, at_tab_sc + EDGE)
+        nc.sync.dma_start(lg_cols[:], lg.rearrange("(p u) -> p u", u=PACK))
+        wgo_dealt = lay("wgo", [P, PACK * S], F32, at_wgo)
+        wgo_rows = wgo.rearrange("(q u) j -> q u j", u=PACK)
+        for start, width in CHUNKS:
+            part = wgo_dealt[:, PACK * start : PACK * (start + width)].rearrange("p (u j) -> p u j", u=PACK)
+            for q in (0, 2, 1, 3):
+                nc.sync.dma_start(part[32 * q : 32 * (q + 1), :, :], wgo_rows[:, :, start : start + width])
 
         w4 = keep.tile([P, PASSES1 * 2 * H], U8, name="w4", align_bytes=64)
         nc.vector.tensor_copy(
-            out=w4[:].bitcast(I32).rearrange("p (ab t g w) -> p ab t g w", t=PACK, g=16, w=4),
-            in_=w4_raw[:].rearrange("p a (b g t w) -> p (a b) t g w", t=PACK, g=16, w=4),
+            out=w4[:].bitcast(I32).rearrange("p (a s g w) -> p s a g w", s=SLICES, g=16, w=4),
+            in_=w4_raw[:].rearrange("p a (g s w) -> p s a g w", s=SLICES, g=16, w=4),
         )
         w4_sc = keep.tile([P, PASSES1 * H], U8, name="w4_sc", align_bytes=64)
         nc.vector.tensor_copy(
-            out=w4_sc[:].bitcast(I32).rearrange("p (ab t g w) -> p ab t g w", t=PACK, g=16, w=2),
-            in_=w4_sc_raw[:].bitcast(I32).rearrange("p (ab g t w) -> p ab t g w", t=PACK, g=16, w=2),
+            out=w4_sc[:].bitcast(I32).rearrange("p (a s g w) -> p s a g w", s=SLICES, g=16, w=2),
+            in_=w4_sc_raw[:].bitcast(I32).rearrange("p (a g s w) -> p s a g w", s=SLICES, g=16, w=2),
         )
 
         v_words = {}
@@ -256,7 +267,7 @@ def tile_list_stain_remix_page_kernel(
             nc.vector.tensor_tensor(
                 out=pages[u][:].indirect(entries(idx2, start, width)),
                 in0=light[c, u][:],
-                in1=wgo_dealt[c][:, u, :],
+                in1=wgo_dealt[:, PACK * start + u * width : PACK * start + (u + 1) * width],
                 op=MULT,
             )
 

@@ -45,8 +45,8 @@ def tile_list_stain_remix_page_kernel(
         def entries(tile, start, width):
             return tile[:, start // 16 : (start + width) // 16]
 
-        at_wr_second = 0
-        at_tab_sc = at_wr_second + 4 * PACK * N - EDGE
+        at_wr = 0
+        at_tab_sc = at_wr + 4 * SLICES * N - EDGE
         at_wgo = at_tab_sc + T - EDGE
 
         def lay(name, shape, dtype, at):
@@ -56,7 +56,7 @@ def tile_list_stain_remix_page_kernel(
         nc.gpsimd.memset(bu_rows[:], 0.0)
         tab_sc = lay("tab_sc", [P, T], U8, at_tab_sc)
         nc.gpsimd.memset(tab_sc[:].bitcast(I32), 0)
-        w4_sc_raw = keep.tile([P, PASSES1 * H], U8, name="w4_sc_raw")
+        w4_sc_raw = keep.tile([P, PASSES1 * H], U8, name="w4_sc_raw", tag="w4_sc_raw", align_bytes=64)
         nc.vector.memset(w4_sc_raw[:].bitcast(I32), 0)
         warm_in = keep.tile([P, 1], F32, name="warm_in")
         warm_out = keep.tile([P, 1], F32, name="warm_out")
@@ -99,14 +99,6 @@ def tile_list_stain_remix_page_kernel(
             )
         load_tab(1)
         load_tab(2)
-        wr_raw = [keep.tile([P, PACK, N], F32, name="wr_raw0"), lay("wr_raw1", [P, PACK, N], F32, at_wr_second)]
-        wr_rows = wr.rearrange("(g s i) n -> s g i n", s=SLICES, i=8)
-
-        def load_wr(b):
-            for t in range(PACK):
-                nc.sync.dma_start(wr_raw[b][:, t, :], wr_rows[PACK * b + t])
-
-        load_wr(0)
         idx2 = keep.tile([P, S // 16], U16, name="idx2")
         nc.sync.dma_start(idx2[:], offs2)
 
@@ -120,7 +112,10 @@ def tile_list_stain_remix_page_kernel(
         for a in range(1, PASSES1):
             nc.sync.dma_start(moved_sc[a - 1][0:112, :].bitcast(I32), got_sc[4 * a : 4 * a + 112, :].bitcast(I32))
         v_scales = [got_sc] + moved_sc
-        load_wr(1)
+        wr_raw = lay("wr_raw", [P, SLICES * N], F32, at_wr)
+        wr_rows = wr.rearrange("(g s i) n -> s g i n", s=SLICES, i=8)
+        for s in range(SLICES):
+            nc.sync.dma_start(wr_raw[:, s * N : (s + 1) * N], wr_rows[s])
         lg_cols = lay("lg_cols", [P, PACK], F32, at_tab_sc + EDGE)
         nc.sync.dma_start(lg_cols[:], lg.rearrange("(p u) -> p u", u=PACK))
         wgo_dealt = lay("wgo", [P, PACK * S], F32, at_wgo)
@@ -143,16 +138,15 @@ def tile_list_stain_remix_page_kernel(
 
         v_words = {}
 
-        def gather(c, a):
-            start, width = CHUNKS[c]
-            tag = {(2, 0): "w4_raw"}.get((c, a), "got%d_%d" % (c, a))
-            if c == 1 and a > 0:
-                width = S - start
-            got = keep.tile([P, width], U32, name="got%d_%d" % (c, a), tag=tag, align_bytes=64)
+        def gather(a, chunks, tag=None):
+            start = CHUNKS[chunks[0]][0]
+            width = sum(CHUNKS[c][1] for c in chunks)
+            name = "got%d_%d" % (a, chunks[0])
+            got = keep.tile([P, width], U32, name=name, tag=tag or name, align_bytes=64)
             nc.vector.tensor_copy(out=got[:], in_=tab[a][:].indirect(entries(idx, start, width)))
-            v_words[c, a] = got[:, 0 : CHUNKS[c][1]]
-            if width > CHUNKS[c][1]:
-                v_words[c + 1, a] = got[:, CHUNKS[c][1] : width]
+            for c in chunks:
+                lo = CHUNKS[c][0] - start
+                v_words[c, a] = got[:, lo : lo + CHUNKS[c][1]]
 
         def unmix_pass(c, a, s, out, first, last):
             start, width = CHUNKS[c]
@@ -178,12 +172,14 @@ def tile_list_stain_remix_page_kernel(
             for s in range(PACK * PASSES2):
                 sums[c, s] = tiles[s // per_bank][:, (s % per_bank) * width : (s % per_bank + 1) * width]
             if per_bank > 1:
-                order = [(a, s) for a in range(PASSES1) for s in range(PACK * PASSES2)]
+                passes = (0, 1, 2) if c == 0 else (2, 0, 1)
+                order = [(a, s) for a in passes for s in range(PACK * PASSES2)]
             else:
                 order = [(a, s) for s in range(PACK * PASSES2) for a in range(PASSES1)]
+            first, last = order[0][0], order[-1][0]
             for a, s in order:
                 unmix_pass(
-                    c, a, s, sums[c, s], a == 0 and s % per_bank == 0, a == PASSES1 - 1 and s % per_bank == per_bank - 1
+                    c, a, s, sums[c, s], a == first and s % per_bank == 0, a == last and s % per_bank == per_bank - 1
                 )
 
         staged = {}
@@ -224,7 +220,7 @@ def tile_list_stain_remix_page_kernel(
             woven = ring.tile([P, N * PACK], BF16, name="woven", tag="woven", align_bytes=64)
             nc.vector.tensor_copy(
                 out=woven[:].rearrange("p (u m t) -> p m t u", u=PACK, t=PACK),
-                in_=wr_raw[b][:].rearrange("p t (m u) -> p m t u", u=PACK),
+                in_=wr_raw[:, b * PACK * N : (b + 1) * PACK * N].rearrange("p (t m u) -> p m t u", t=PACK, u=PACK),
             )
             wr_q[b] = quantise(woven, N, "wr%d" % b)
 
@@ -271,13 +267,13 @@ def tile_list_stain_remix_page_kernel(
                 op=MULT,
             )
 
-        for a in range(PASSES1):
-            gather(0, a)
+        gather(0, [0, 1])
+        gather(1, [0, 1, 2], "w4_sc_raw")
+        gather(2, [0])
+        gather(2, [1, 2])
         unmix(0, [0, 1, 2, 3])
-        for a in range(PASSES1):
-            gather(1, a)
         unmix(1, [4, 5, 6, 7])
-        gather(2, 0)
+        gather(0, [2], "w4_raw")
         for b in range(PASSES2):
             prepare_wr(b)
             rectify(0, b)

@@ -126,14 +126,14 @@ def tile_list_stain_remix_page_kernel(
                 nc.sync.dma_start(part[32 * q : 32 * (q + 1), :, :], wgo_rows[:, :, start : start + width])
 
         w4 = keep.tile([P, PASSES1 * 2 * H], U8, name="w4", align_bytes=64)
-        nc.vector.tensor_copy(
-            out=w4[:].bitcast(I32).rearrange("p (a s g w) -> p s a g w", s=SLICES, g=16, w=4),
-            in_=w4_raw[:].rearrange("p a (g s w) -> p s a g w", s=SLICES, g=16, w=4),
+        nc.scalar.copy(
+            out=w4[:].bitcast(U32).rearrange("p (a s g w) -> p s a g w", s=SLICES, g=16, w=4),
+            in_=w4_raw[:].bitcast(U32).rearrange("p a (g s w) -> p s a g w", s=SLICES, g=16, w=4),
         )
         w4_sc = keep.tile([P, PASSES1 * H], U8, name="w4_sc", align_bytes=64)
-        nc.vector.tensor_copy(
-            out=w4_sc[:].bitcast(I32).rearrange("p (a s g w) -> p s a g w", s=SLICES, g=16, w=2),
-            in_=w4_sc_raw[:].bitcast(I32).rearrange("p (a g s w) -> p s a g w", s=SLICES, g=16, w=2),
+        nc.scalar.copy(
+            out=w4_sc[:].bitcast(U32).rearrange("p (a s g w) -> p s a g w", s=SLICES, g=16, w=2),
+            in_=w4_sc_raw[:].bitcast(U32).rearrange("p (a g s w) -> p s a g w", s=SLICES, g=16, w=2),
         )
 
         v_words = {}

@@ -48,6 +48,7 @@ def tile_list_stain_remix_page_kernel(
         at_wr = 0
         at_tab_sc = at_wr + 4 * SLICES * N - EDGE
         at_wgo = at_tab_sc + T - EDGE
+        at_tab0 = at_wgo + 4 * PACK * S
 
         def lay(name, shape, dtype, at):
             return laid.tile(shape, dtype, name=name, align_bytes=EDGE, offset=at)
@@ -63,9 +64,11 @@ def tile_list_stain_remix_page_kernel(
         nc.vector.memset(warm_in[:], 0.0)
         ident = keep.tile([P, P], F32, name="ident")
         make_identity(nc, ident[:])
-        moved_sc = [keep.tile([P, S], U8, name="moved_sc%d" % a, align_bytes=64) for a in range(1, PASSES1)]
-        for plane in moved_sc:
-            nc.gpsimd.memset(plane[:].bitcast(I32), 0)
+        moved_sc = {}
+        for h in range(2):
+            for a in range(1, PASSES1):
+                moved_sc[a, h] = keep.tile([P, BANK], U8, name="moved_sc%d_%d" % (a, h), align_bytes=64)
+                nc.gpsimd.memset(moved_sc[a, h][:].bitcast(I32), 0)
         pages = [keep.tile([P, T2], F32, name="page%d" % u) for u in range(PACK)]
         for page in pages[:2]:
             nc.vector.memset(page[:, 0:1023], 0.0)
@@ -76,7 +79,10 @@ def tile_list_stain_remix_page_kernel(
 
         idx = keep.tile([P, S // 16], U16, name="idx")
         nc.sync.dma_start(idx[:], offs)
-        tab = [keep.tile([P, T], U32, name="tab%d" % a) for a in range(PASSES1)]
+        idx2 = keep.tile([P, S // 16], U16, name="idx2")
+        nc.sync.dma_start(idx2[:], offs2)
+        tab = [lay("tab0", [P, T], U32, at_tab0)]
+        tab.extend(keep.tile([P, T], U32, name="tab%d" % a) for a in range(1, PASSES1))
 
         def load_tab(a):
             nc.sync.dma_start(tab[a][:].bitcast(I32), tab_words[a].rearrange("p t i -> p (t i)").bitcast(I32))
@@ -99,23 +105,44 @@ def tile_list_stain_remix_page_kernel(
             )
         load_tab(1)
         load_tab(2)
-        idx2 = keep.tile([P, S // 16], U16, name="idx2")
-        nc.sync.dma_start(idx2[:], offs2)
 
         bu_bank = bank(7)
         nc.tensor.transpose(bu_bank[:, 0:P], bu_rows[:], ident[:])
         bu_cols = keep.tile([P, PACK * PASSES2], F32, name="bu_cols")
         nc.scalar.copy(out=bu_cols[:], in_=bu_bank[:, 0 : PACK * PASSES2])
 
-        got_sc = keep.tile([P, S], U8, name="got_sc", align_bytes=64)
-        nc.vector.tensor_copy(out=got_sc[:], in_=tab_sc[:].indirect(idx[:]))
-        for a in range(1, PASSES1):
-            nc.sync.dma_start(moved_sc[a - 1][0:112, :].bitcast(I32), got_sc[4 * a : 4 * a + 112, :].bitcast(I32))
-        v_scales = [got_sc] + moved_sc
+        v_words = {}
+
+        def gather(a, chunks, tag=None):
+            start = CHUNKS[chunks[0]][0]
+            width = sum(CHUNKS[c][1] for c in chunks)
+            name = "got%d_%d" % (a, chunks[0])
+            got = keep.tile([P, width], U32, name=name, tag=tag or name, align_bytes=64)
+            nc.vector.tensor_copy(out=got[:], in_=tab[a][:].indirect(entries(idx, start, width)))
+            for c in chunks:
+                lo = CHUNKS[c][0] - start
+                v_words[c, a] = got[:, lo : lo + CHUNKS[c][1]]
+
+        gather(0, [0, 1, 2])
+
+        got_sc = [lay("got_sc%d" % h, [P, BANK], U8, at_tab0 + h * BANK) for h in range(2)]
+
+        def shift(h):
+            for a in range(1, PASSES1):
+                nc.sync.dma_start(moved_sc[a, h][0:112, :].bitcast(I32), got_sc[h][4 * a : 4 * a + 112, :].bitcast(I32))
+
+        def v_scales(a, lo, hi):
+            plane = moved_sc[a, lo // BANK] if a else got_sc[lo // BANK]
+            return plane[:, lo % BANK : lo % BANK + hi - lo]
+
+        for h in range(2):
+            nc.vector.tensor_copy(out=got_sc[h][:], in_=tab_sc[:].indirect(entries(idx, h * BANK, BANK)))
+        shift(0)
         wr_raw = lay("wr_raw", [P, SLICES * N], F32, at_wr)
         wr_rows = wr.rearrange("(g s i) n -> s g i n", s=SLICES, i=8)
         for s in range(SLICES):
             nc.sync.dma_start(wr_raw[:, s * N : (s + 1) * N], wr_rows[s])
+        shift(1)
         lg_cols = lay("lg_cols", [P, PACK], F32, at_tab_sc + EDGE)
         nc.sync.dma_start(lg_cols[:], lg.rearrange("(p u) -> p u", u=PACK))
         wgo_dealt = lay("wgo", [P, PACK * S], F32, at_wgo)
@@ -136,18 +163,6 @@ def tile_list_stain_remix_page_kernel(
             in_=w4_sc_raw[:].bitcast(U32).rearrange("p (a g s w) -> p s a g w", s=SLICES, g=16, w=2),
         )
 
-        v_words = {}
-
-        def gather(a, chunks, tag=None):
-            start = CHUNKS[chunks[0]][0]
-            width = sum(CHUNKS[c][1] for c in chunks)
-            name = "got%d_%d" % (a, chunks[0])
-            got = keep.tile([P, width], U32, name=name, tag=tag or name, align_bytes=64)
-            nc.vector.tensor_copy(out=got[:], in_=tab[a][:].indirect(entries(idx, start, width)))
-            for c in chunks:
-                lo = CHUNKS[c][0] - start
-                v_words[c, a] = got[:, lo : lo + CHUNKS[c][1]]
-
         def unmix_pass(c, a, s, out, first, last):
             start, width = CHUNKS[c]
             step = BANK if width == BANK else P
@@ -158,7 +173,7 @@ def tile_list_stain_remix_page_kernel(
                     lhsT=w4[:, 2 * col : 2 * (col + P)].bitcast(E2M1),
                     lhsT_scale=w4_sc[:, col : col + P],
                     rhs=v_words[c, a][:, j : j + step].bitcast(E4M3),
-                    rhs_scale=v_scales[a][:, start + j : start + j + step],
+                    rhs_scale=v_scales(a, start + j, start + j + step),
                     start=first and j == 0,
                     stop=last and j + step == width,
                 )
@@ -173,7 +188,9 @@ def tile_list_stain_remix_page_kernel(
                 sums[c, s] = tiles[s // per_bank][:, (s % per_bank) * width : (s % per_bank + 1) * width]
             if per_bank > 1:
                 passes = (0, 1, 2) if c == 0 else (2, 0, 1)
-                order = [(a, s) for a in passes for s in range(PACK * PASSES2)]
+                order = [(passes[0], s) for s in range(SLICES)]
+                for low in range(0, SLICES, per_bank):
+                    order.extend((a, s) for a in passes[1:] for s in range(low, low + per_bank))
             else:
                 order = [(a, s) for s in range(PACK * PASSES2) for a in range(PASSES1)]
             first, last = order[0][0], order[-1][0]
@@ -267,13 +284,11 @@ def tile_list_stain_remix_page_kernel(
                 op=MULT,
             )
 
-        gather(0, [0, 1])
         gather(1, [0, 1, 2], "w4_sc_raw")
         gather(2, [0])
         gather(2, [1, 2])
         unmix(0, [0, 1, 2, 3])
         unmix(1, [4, 5, 6, 7])
-        gather(0, [2], "w4_raw")
         for b in range(PASSES2):
             prepare_wr(b)
             rectify(0, b)

from contextlib import ExitStack

import concourse.mybir as mybir
from concourse.masks import make_identity

K, T, S, H, N, T2, P = 1536, 2048, 1024, 1024, 512, 2048, 128
FLOPS = 2 * K * H * S + 2 * H * N * S

F32 = mybir.dt.float32
BF16 = mybir.dt.bfloat16
I32 = mybir.dt.int32
U32 = mybir.dt.uint32
U16 = mybir.dt.uint16
U8 = mybir.dt.uint8
E4M3 = mybir.dt.float8_e4m3fn_x4
E2M1 = mybir.dt.float4_e2m1fn_x4
ACT = mybir.ActivationFunctionType
MULT = mybir.AluOpType.mult

PACK = 4
KP = P * PACK
PASSES1 = K // KP
PASSES2 = H // KP
BANK = 512
CHUNKS = [(0, 256), (256, 256), (512, 512)]
QUARTER = T2 // 4
EIGHTH = T2 // 8
SLICES = PACK * PASSES2
EDGE = 64


def tile_list_stain_remix_page_kernel(
    tc, tab_words, tab_scales, offs, w4_words, w4_scales, bu, wr, lg, wgo, offs2, out_0, out_1, out_2
):
    nc = tc.nc
    with ExitStack() as ctx:
        keep = ctx.enter_context(tc.tile_pool(name="keep", bufs=1))
        laid = ctx.enter_context(tc.tile_pool(name="laid", bufs=1))
        ring = ctx.enter_context(tc.tile_pool(name="ring", bufs=4))
        psum = ctx.enter_context(tc.psum_pool(name="psum", bufs=1))

        def bank(i):
            return psum.tile([P, BANK], F32, name="bank%d" % i, tag="bank%d" % i)

        def entries(tile, start, width):
            return tile[:, start // 16 : (start + width) // 16]

        at_wr = 0
        at_tab_sc = at_wr + 4 * SLICES * N - EDGE
        at_wgo = at_tab_sc + T - EDGE
        at_tab0 = at_wgo + 4 * PACK * S

        def lay(name, shape, dtype, at):
            return laid.tile(shape, dtype, name=name, align_bytes=EDGE, offset=at)

        bu_rows = keep.tile([P, P], F32, name="bu_rows")
        nc.gpsimd.memset(bu_rows[:], 0.0)
        tab_sc = lay("tab_sc", [P, T], U8, at_tab_sc)
        nc.gpsimd.memset(tab_sc[:].bitcast(I32), 0)
        w4_sc_raw = keep.tile([P, PASSES1 * H], U8, name="w4_sc_raw", tag="w4_sc_raw", align_bytes=64)
        nc.vector.memset(w4_sc_raw[:].bitcast(I32), 0)
        warm_in = keep.tile([P, 1], F32, name="warm_in")
        warm_out = keep.tile([P, 1], F32, name="warm_out")
        nc.vector.memset(warm_in[:], 0.0)
        ident = keep.tile([P, P], F32, name="ident")
        make_identity(nc, ident[:])
        moved_sc = {}
        for h in range(2):
            for a in range(1, PASSES1):
                moved_sc[a, h] = keep.tile([P, BANK], U8, name="moved_sc%d_%d" % (a, h), align_bytes=64)
                nc.gpsimd.memset(moved_sc[a, h][:].bitcast(I32), 0)
        pages = [keep.tile([P, T2], F32, name="page%d" % u) for u in range(PACK)]
        for page in pages[:2]:
            nc.vector.memset(page[:, 0:1023], 0.0)
            nc.vector.memset(page[:, 1023:T2], 0.0)
        for page in pages[2:]:
            for half in range(2):
                nc.gpsimd.memset(page[:, half * 1024 : (half + 1) * 1024], 0.0)

        idx = keep.tile([P, S // 16], U16, name="idx")
        nc.sync.dma_start(idx[:], offs)
        idx2 = keep.tile([P, S // 16], U16, name="idx2")
        nc.sync.dma_start(idx2[:], offs2)
        tab = [lay("tab0", [P, T], U32, at_tab0)]
        tab.extend(keep.tile([P, T], U32, name="tab%d" % a) for a in range(1, PASSES1))

        def load_tab(a):
            nc.sync.dma_start(tab[a][:].bitcast(I32), tab_words[a].rearrange("p t i -> p (t i)").bitcast(I32))

        load_tab(0)
        nc.scalar.dma_start(
            bu_rows[0:SLICES, :].rearrange("s (g i) -> s g i", i=8), bu.rearrange("(g s i) -> s g i", s=SLICES, i=8)
        )
        for q in range(4):
            nc.scalar.dma_start(
                tab_sc[32 * q : 32 * q + 4 * PASSES1, :].bitcast(I32), tab_scales[:, 4 * q : 4 * q + 4, :].bitcast(I32)
            )
        nc.scalar.activation(out=warm_out[:], in_=warm_in[:], func=ACT.Exp)
        w4_raw = keep.tile([P, PASSES1, H // 2], I32, name="w4_raw", align_bytes=64)
        nc.sync.dma_start(w4_raw[:], w4_words.bitcast(I32).rearrange("a p w -> p a w"))
        for q in range(4):
            nc.sync.dma_start(
                w4_sc_raw[32 * q : 32 * q + 4, :].bitcast(I32).rearrange("r (a w) -> r a w", a=PASSES1),
                w4_scales[:, 4 * q : 4 * q + 4, :].bitcast(I32).rearrange("a r w -> r a w"),
            )
        load_tab(1)
        load_tab(2)

        bu_bank = bank(7)
        nc.tensor.transpose(bu_bank[:, 0:P], bu_rows[:], ident[:])
        bu_cols = keep.tile([P, PACK * PASSES2], F32, name="bu_cols")
        nc.scalar.copy(out=bu_cols[:], in_=bu_bank[:, 0 : PACK * PASSES2])

        v_words = {}

        def gather(a, chunks, tag=None):
            start = CHUNKS[chunks[0]][0]
            width = sum(CHUNKS[c][1] for c in chunks)
            name = "got%d_%d" % (a, chunks[0])
            got = keep.tile([P, width], U32, name=name, tag=tag or name, align_bytes=64)
            nc.vector.tensor_copy(out=got[:], in_=tab[a][:].indirect(entries(idx, start, width)))
            for c in chunks:
                lo = CHUNKS[c][0] - start
                v_words[c, a] = got[:, lo : lo + CHUNKS[c][1]]

        gather(0, [0, 1, 2])

        got_sc = [lay("got_sc%d" % h, [P, BANK], U8, at_tab0 + h * BANK) for h in range(2)]

        def shift(h):
            for a in range(1, PASSES1):
                nc.sync.dma_start(moved_sc[a, h][0:112, :].bitcast(I32), got_sc[h][4 * a : 4 * a + 112, :].bitcast(I32))

        def v_scales(a, lo, hi):
            plane = moved_sc[a, lo // BANK] if a else got_sc[lo // BANK]
            return plane[:, lo % BANK : lo % BANK + hi - lo]

        for h in range(2):
            nc.vector.tensor_copy(out=got_sc[h][:], in_=tab_sc[:].indirect(entries(idx, h * BANK, BANK)))
        shift(0)
        wr_raw = lay("wr_raw", [P, SLICES * N], F32, at_wr)
        wr_rows = wr.rearrange("(g s i) n -> s g i n", s=SLICES, i=8)
        for s in range(SLICES):
            nc.sync.dma_start(wr_raw[:, s * N : (s + 1) * N], wr_rows[s])
        shift(1)
        lg_cols = lay("lg_cols", [P, PACK], F32, at_tab_sc + EDGE)
        nc.sync.dma_start(lg_cols[:], lg.rearrange("(p u) -> p u", u=PACK))
        wgo_dealt = lay("wgo", [P, PACK * S], F32, at_wgo)
        wgo_rows = wgo.rearrange("(q u) j -> q u j", u=PACK)
        for start, width in CHUNKS:
            part = wgo_dealt[:, PACK * start : PACK * (start + width)].rearrange("p (u j) -> p u j", u=PACK)
            for q in (0, 2, 1, 3):
                nc.sync.dma_start(part[32 * q : 32 * (q + 1), :, :], wgo_rows[:, :, start : start + width])

        w4 = keep.tile([P, PASSES1 * 2 * H], U8, name="w4", align_bytes=64)
        nc.scalar.copy(
            out=w4[:].bitcast(U32).rearrange("p (a s g w) -> p s a g w", s=SLICES, g=16, w=4),
            in_=w4_raw[:].bitcast(U32).rearrange("p a (g s w) -> p s a g w", s=SLICES, g=16, w=4),
        )
        w4_sc = keep.tile([P, PASSES1 * H], U8, name="w4_sc", align_bytes=64)
        nc.scalar.copy(
            out=w4_sc[:].bitcast(U32).rearrange("p (a s g w) -> p s a g w", s=SLICES, g=16, w=2),
            in_=w4_sc_raw[:].bitcast(U32).rearrange("p (a g s w) -> p s a g w", s=SLICES, g=16, w=2),
        )

        def unmix_pass(c, a, s, out, first, last):
            start, width = CHUNKS[c]
            step = BANK if width == BANK else P
            col = a * H + s * P
            for j in range(0, width, step):
                nc.tensor.matmul_mx(
                    out=out[:, j : j + step],
                    lhsT=w4[:, 2 * col : 2 * (col + P)].bitcast(E2M1),
                    lhsT_scale=w4_sc[:, col : col + P],
                    rhs=v_words[c, a][:, j : j + step].bitcast(E4M3),
                    rhs_scale=v_scales(a, start + j, start + j + step),
                    start=first and j == 0,
                    stop=last and j + step == width,
                )

        sums = {}

        def unmix(c, banks):
            width = CHUNKS[c][1]
            per_bank = BANK // width
            tiles = [bank(i) for i in banks]
            for s in range(PACK * PASSES2):
                sums[c, s] = tiles[s // per_bank][:, (s % per_bank) * width : (s % per_bank + 1) * width]
            if per_bank > 1:
                passes = (0, 1, 2) if c == 0 else (2, 0, 1)
                order = [(passes[0], s) for s in range(SLICES)]
                for low in range(0, SLICES, per_bank):
                    order.extend((a, s) for a in passes[1:] for s in range(low, low + per_bank))
            else:
                order = [(a, s) for s in range(PACK * PASSES2) for a in range(PASSES1)]
            first, last = order[0][0], order[-1][0]
            for a, s in order:
                unmix_pass(
                    c, a, s, sums[c, s], a == first and s % per_bank == 0, a == last and s % per_bank == per_bank - 1
                )

        staged = {}

        def rectify(c, b):
            width = CHUNKS[c][1]
            if (c, b) == (2, 1):
                stage = keep.tile([P, PACK, width], BF16, name="held", tag="held")
            else:
                stage = ring.tile([P, PACK, width], BF16, name="stage", tag="stage")
            for t in range(PACK):
                s = PACK * b + t
                nc.scalar.activation(out=stage[:, t, :], in_=sums[c, s], func=ACT.Relu, bias=bu_cols[:, s : s + 1])
            staged[c, b] = stage

        def weave(engine, stage, width, tag=None):
            if tag:
                woven = keep.tile([P, width * PACK], BF16, name="woven_" + tag, tag=tag, align_bytes=64)
            else:
                woven = ring.tile([P, width * PACK], BF16, name="woven", tag="woven", align_bytes=64)
            dst = woven[:].rearrange("p (c i t) -> p c t i", i=4, t=PACK)
            src = stage[:].rearrange("p t (c i) -> p c t i", i=4)
            if engine == "vector":
                nc.vector.tensor_copy(out=dst, in_=src)
            else:
                nc.scalar.copy(out=dst, in_=src)
            return woven

        def quantise(woven, width, name, tag=None):
            codes = keep.tile([P, width], U32, name=name + "_codes", tag=name + "_codes", align_bytes=64)
            scales = keep.tile([P, width], U8, name=name + "_scales", tag=tag or name + "_scales", align_bytes=64)
            nc.vector.quantize_mx(out=codes[:].bitcast(E4M3), scales=scales[:], in_=woven[:])
            return codes, scales

        wr_q = {}

        def prepare_wr(b):
            woven = ring.tile([P, N * PACK], BF16, name="woven", tag="woven", align_bytes=64)
            nc.vector.tensor_copy(
                out=woven[:].rearrange("p (u m t) -> p m t u", u=PACK, t=PACK),
                in_=wr_raw[:, b * PACK * N : (b + 1) * PACK * N].rearrange("p (t m u) -> p m t u", t=PACK, u=PACK),
            )
            wr_q[b] = quantise(woven, N, "wr%d" % b)

        c_q = {}

        def quantise_c(c, b, engine):
            width = CHUNKS[c][1]
            woven = weave(engine, staged[c, b], width, {(2, 1): "last"}.get((c, b)))
            c_q[c, b] = quantise(woven, width, "c%d_%d" % (c, b))

        light = {}

        def remix(c, banks):
            width = CHUNKS[c][1]
            per_bank = BANK // width
            tiles = [bank(i) for i in banks]
            for u in range(PACK):
                d = tiles[u // per_bank][:, (u % per_bank) * width : (u % per_bank + 1) * width]
                for b in range(PASSES2):
                    nc.tensor.matmul_mx(
                        out=d,
                        lhsT=wr_q[b][0][:, u * P : (u + 1) * P].bitcast(E4M3),
                        lhsT_scale=wr_q[b][1][:, u * P : (u + 1) * P],
                        rhs=c_q[c, b][0][:].bitcast(E4M3),
                        rhs_scale=c_q[c, b][1][:],
                        start=b == 0,
                        stop=b == PASSES2 - 1,
                    )
                sums["d", c, u] = d

        def transmit(c, u):
            width = CHUNKS[c][1]
            tag = {(1, 3): "held", (1, 2): "last"}.get((c, u), "y%d_%d" % (c, u))
            y = keep.tile([P, width], F32, name="y%d_%d" % (c, u), tag=tag, align_bytes=None if tag == "held" else 64)
            nc.scalar.activation(out=y[:], in_=sums["d", c, u], func=ACT.Exp, scale=-1.0, bias=lg_cols[:, u : u + 1])
            light[c, u] = y

        def scatter(c, u):
            start, width = CHUNKS[c]
            nc.vector.tensor_tensor(
                out=pages[u][:].indirect(entries(idx2, start, width)),
                in0=light[c, u][:],
                in1=wgo_dealt[:, PACK * start + u * width : PACK * start + (u + 1) * width],
                op=MULT,
            )

        gather(1, [0, 1, 2], "w4_sc_raw")
        gather(2, [0])
        gather(2, [1, 2])
        unmix(0, [0, 1, 2, 3])
        unmix(1, [4, 5, 6, 7])
        for b in range(PASSES2):
            prepare_wr(b)
            rectify(0, b)
            quantise_c(0, b, "vector")
        remix(0, [0, 1])
        for u in range(PACK):
            transmit(0, u)
            scatter(0, u)
        for b in range(PASSES2):
            rectify(1, b)
            quantise_c(1, b, "vector")
        unmix(2, [2, 3, 4, 5, 6, 7, 0, 1])
        rectify(2, 0)
        remix(1, [2, 3])
        for u in range(2):
            transmit(1, u)
            scatter(1, u)
        quantise_c(2, 0, "scalar")
        rectify(2, 1)
        quantise_c(2, 1, "scalar")
        remix(2, [4, 5, 6, 7])
        for u in (3, 2):
            transmit(1, u)
            scatter(1, u)

        out_rows = out_0.rearrange("(p u) m -> p u m", u=PACK)
        pairs = [ring.tile([P, 2, QUARTER, 2], BF16, name="stage", tag="stage") for q in range(4)]
        for u in range(PACK):
            transmit(2, u)
            scatter(2, u)
        for u in range(PACK):
            nc.sync.dma_start(out_rows[:, u, :], pages[u][:])
            for q in range(4):
                cuts = [(0, EIGHTH), (EIGHTH, QUARTER)] if u >= 2 and q == 0 else [(0, QUARTER)]
                for lo, hi in cuts:
                    copy = nc.vector.tensor_copy if hi == EIGHTH else nc.scalar.copy
                    copy(out=pairs[q][:, u // 2, lo:hi, u % 2], in_=pages[u][:, q * QUARTER + lo : q * QUARTER + hi])

        out_words = out_1[0].rearrange("p m t -> p (m t)").bitcast(I32)
        y_scales = keep.tile([P, T2], U8, name="y_scales", align_bytes=64)
        page_woven = []
        for q in range(4):
            woven = ring.tile([P, QUARTER * PACK], BF16, name="woven", tag="woven", align_bytes=64)
            words = pairs[q][:].rearrange("p h m e -> p (h m e)")
            copy, word = (nc.vector.tensor_copy, I32) if q < 3 else (nc.scalar.copy, U32)
            for lo, hi in [(0, QUARTER)] if q in (1, 2) else [(0, EIGHTH), (EIGHTH, QUARTER)]:
                copy(
                    out=woven[:].bitcast(word).rearrange("p (m h) -> p m h", h=2)[:, lo:hi, :],
                    in_=words.bitcast(word).rearrange("p (h m) -> p m h", h=2)[:, lo:hi, :],
                )
            page_woven.append(woven)
        for q in range(4):
            for lo, hi in [(0, QUARTER)] if q < 3 else [(0, EIGHTH), (EIGHTH, QUARTER)]:
                cols = slice(q * QUARTER + lo, q * QUARTER + hi)
                y_codes = keep.tile([P, hi - lo], U32, name="y_codes%d_%d" % (q, lo), align_bytes=64)
                nc.vector.quantize_mx(
                    out=y_codes[:].bitcast(E4M3), scales=y_scales[:, cols], in_=page_woven[q][:, PACK * lo : PACK * hi]
                )
                nc.sync.dma_start(out_words[:, cols], y_codes[:].bitcast(I32))
        for q in range(4):
            queue = nc.sync if q % 2 == 0 else nc.scalar
            queue.dma_start(out_2[0, 4 * q : 4 * q + 4, :].bitcast(I32), y_scales[32 * q : 32 * q + 4, :].bitcast(I32))
